import numpy as np
import ml_dtypes


def mxq(x, axis, fmt="e4m3"):
    dtype, down = {"e4m3": (ml_dtypes.float8_e4m3fn, 7), "e5m2": (ml_dtypes.float8_e5m2, 14)}[fmt]
    v = np.moveaxis(np.asarray(x, np.float32).astype(ml_dtypes.bfloat16).astype(np.float64), axis, -1)
    blocks = v.reshape(v.shape[:-1] + (-1, 32))
    amax = np.abs(blocks).max(-1, keepdims=True)
    byte = np.maximum(np.where(amax > 0, np.frexp(amax)[1] - 1 + 127, 0) - down, 1)
    scale = np.exp2(byte - 127.0)
    codes = (blocks / scale).astype(np.float32).astype(dtype).astype(np.float64)
    return np.moveaxis((codes * scale).reshape(v.shape), -1, axis)


WIDE = False


def mx_kscale(k):
    if not WIDE:
        return np.ones(k)
    levels = np.array([30, -30])
    if k % 512:
        return np.exp2(np.random.permutation(np.resize(levels, k // 32))).repeat(32)
    a = np.empty((k // 512, 16))
    for p in range(k // 512):
        a[p, :8] = np.random.permutation(np.resize(levels, 8))
        for g in range(8):
            far = levels[np.abs(levels - a[p, g]) >= 10]
            a[p, g + 8] = far[np.random.randint(len(far))]
    return np.exp2(a.ravel()).repeat(32)


def f64(x):
    return np.asarray(x).astype(np.float64)


def striped(idx):
    return np.tile(np.asarray(idx).reshape(-1, 16).T, (8, 1)).astype(np.uint16)


def unstriped(offs):
    return offs[:16].T.reshape(-1).astype(np.int64)


E2M1 = np.array([0.0, 0.5, 1.0, 1.5, 2.0, 3.0, 4.0, 6.0, -0.0, -0.5, -1.0, -1.5, -2.0, -3.0, -4.0, -6.0])


def pack_weight(w, fmt):
    k, n = w.shape
    w = f64(np.asarray(w, np.float32).astype(ml_dtypes.bfloat16)).reshape(k // 32, 32, n)
    amax = np.abs(w).max(1)
    if fmt in ("e4m3", "e5m2"):
        byte = np.frexp(amax)[1] - 1 + 127 - (7 if fmt == "e4m3" else 14)
    else:
        mant, ex = np.frexp(amax / 6.0)
        byte = np.where(mant > 0.5, ex, ex - 1) + 127
    byte = np.clip(np.where(amax > 0, byte, 1), 1, 254)
    scaled = (w * np.exp2(127.0 - byte)[:, None, :]).reshape(k, n).astype(np.float32)
    by_word = np.ascontiguousarray(scaled.reshape(k // 512, 128, 4, n).transpose(0, 1, 3, 2))
    if fmt in ("e4m3", "e5m2"):
        words = by_word.astype(ml_dtypes.float8_e4m3fn if fmt == "e4m3" else ml_dtypes.float8_e5m2).view(np.uint8)
    else:
        c = by_word.astype(ml_dtypes.float4_e2m1fn).view(np.uint8) & 0xF
        words = (c[..., 0::2] | (c[..., 1::2] << 4)).reshape(k // 512, 128, 2 * n)
    return np.ascontiguousarray(words), np.ascontiguousarray(byte.astype(np.uint8).reshape(k // 512, 16, n))


def unpack_weight(words, scales, fmt):
    g, _, n = scales.shape
    words = np.ascontiguousarray(words).reshape(g, 128, n, -1)
    if fmt in ("e4m3", "e5m2"):
        vals = words.view(ml_dtypes.float8_e4m3fn if fmt == "e4m3" else ml_dtypes.float8_e5m2).astype(np.float64)
    else:
        nib = np.empty((g, 128, n, 4), np.uint8)
        nib[..., 0::2] = words & 0xF
        nib[..., 1::2] = words >> 4
        vals = E2M1[nib]
    vals = vals * np.repeat(np.exp2(scales.astype(np.float64) - 127.0), 8, axis=1)[..., None]
    return vals.transpose(0, 1, 3, 2).reshape(g * 512, n)


K, T, J, R, O, N, L, E = 512, 2048, 256, 512, 128, 256, 512, 1024


def setup_inputs():
    n = np.random.standard_normal
    idx = np.random.permutation(T)[:J]
    idx2 = np.random.permutation(T)[:J]
    idx3 = np.random.permutation(J)[:O]
    idx4 = np.random.permutation(J)[:O]
    idx5 = np.random.permutation(E)[:O]
    fk = mx_kscale(K)
    fr = mx_kscale(R)
    fl = mx_kscale(L)
    xtp = pack_weight(n((K, T)) / fk[:, None], "e5m2")
    wp = pack_weight(n((K, R)) * 1 / np.sqrt(K) * fk[:, None] * fr, "e2m1")
    wbp = pack_weight(n((R, N)) * 1 / np.sqrt(R) / fr[:, None], "e2m1")
    sxp = pack_weight(n((L, O)) / fl[:, None], "e4m3")
    wsp = pack_weight(n((L, N)) * 1 / np.sqrt(L) * fl[:, None], "e2m1")
    return {
        "xt_words": xtp[0],
        "xt_scales": xtp[1],
        "w_words": wp[0],
        "w_scales": wp[1],
        "wb_words": wbp[0],
        "wb_scales": wbp[1],
        "sx_words": sxp[0],
        "sx_scales": sxp[1],
        "ws_words": wsp[0],
        "ws_scales": wsp[1],
        "offs": striped(idx),
        "offs2": striped(idx2),
        "offs3": striped(idx3),
        "offs4": striped(idx4),
        "offs5": striped(idx5),
    }


def reference(xt_words, xt_scales, w_words, w_scales, wb_words, wb_scales, sx_words, sx_scales, ws_words, ws_scales, offs, offs2, offs3, offs4, offs5):
    idx = unstriped(offs)
    idx2 = unstriped(offs2)
    idx3 = unstriped(offs3)
    idx4 = unstriped(offs4)
    idx5 = unstriped(offs5)
    xtu = unpack_weight(xt_words, xt_scales, "e5m2")
    wu = unpack_weight(w_words, w_scales, "e2m1")
    wbu = unpack_weight(wb_words, wb_scales, "e2m1")
    sxu = unpack_weight(sx_words, sx_scales, "e4m3")
    wsu = unpack_weight(ws_words, ws_scales, "e2m1")
    xtidxg = xtu[:, idx]
    a = wu.T @ xtidxg
    xtidx2g = xtu[:, idx2]
    b = wu.T @ xtidx2g
    hid = np.abs(a[:, idx3] - b[:, idx4])
    hidq = mxq(hid, 0, "e4m3")
    p = wbu.T @ hidq + wsu.T @ sxu
    y = np.zeros((N, E))
    y[:, idx5] = p
    return y

@@ -1,0 +1,166 @@
+from contextlib import ExitStack
+
+import concourse.mybir as mybir
+
+K, T, J, R, O, N, L, E = 512, 2048, 256, 512, 128, 256, 512, 1024
+FLOPS = 2 * (2 * K * R * J + R * N * O + L * N * O)
+
+F32 = mybir.dt.float32
+BF16 = mybir.dt.bfloat16
+I32 = mybir.dt.int32
+U32 = mybir.dt.uint32
+U16 = mybir.dt.uint16
+U8 = mybir.dt.uint8
+E4M3 = mybir.dt.float8_e4m3fn_x4
+E5M2 = mybir.dt.float8_e5m2_x4
+E2M1 = mybir.dt.float4_e2m1fn_x4
+ACT = mybir.ActivationFunctionType
+ALU = mybir.AluOpType
+
+P = 128
+PACK = 4
+
+
+def tile_list_tied_looked_skip_scattered_kernel(
+    tc, xt_words, xt_scales, w_words, w_scales, wb_words, wb_scales, sx_words, sx_scales,
+    ws_words, ws_scales, offs, offs2, offs3, offs4, offs5, out,
+):
+    nc = tc.nc
+    with ExitStack() as ctx:
+        lists = ctx.enter_context(tc.tile_pool(name="lists", bufs=1))
+        sb = ctx.enter_context(tc.tile_pool(name="sb", bufs=1))
+        psum = ctx.enter_context(tc.psum_pool(name="psum", bufs=1))
+
+        def load_list(src, name):
+            tile = lists.tile(list(src.shape), U16, name=name)
+            nc.sync.dma_start(tile[:], src)
+            return tile
+
+        def load_words(queue, src, name, dtype):
+            flat = src.bitcast(I32)
+            per_word = 1 if dtype == U32 else 4
+            tile = sb.tile([P, flat.shape[1] * per_word], dtype, name=name, align_bytes=64)
+            queue.dma_start(tile[:].bitcast(I32), flat)
+            return tile
+
+        def scale_tile(engine, src, name):
+            tile = sb.tile([P, src.shape[2]], U8, name=name, align_bytes=64)
+            engine.memset(tile[:].bitcast(I32), 0)
+            return tile
+
+        def load_scales(queues, tile, src):
+            for q in range(4):
+                queues[q].dma_start(tile[32 * q : 32 * q + 4, :].bitcast(I32), src[0, 4 * q : 4 * q + 4, :].bitcast(I32))
+
+        sync4 = [nc.sync] * 4
+        xt_plane = scale_tile(nc.vector, xt_scales, "xt_plane")
+        w_plane = scale_tile(nc.vector, w_scales, "w_plane")
+        idx = load_list(offs, "idx")
+        w_raw = load_words(nc.sync, w_words[0], "w_raw", U8)
+        idx2 = load_list(offs2, "idx2")
+        load_scales([nc.sync, nc.sync, nc.scalar, nc.scalar], xt_plane, xt_scales)
+        xt = load_words(nc.sync, xt_words[0].rearrange("p c r -> p (c r)"), "xt", U32)
+        load_scales(sync4, w_plane, w_scales)
+        idx3 = load_list(offs3, "idx3")
+        idx4 = load_list(offs4, "idx4")
+
+        ws_plane = scale_tile(nc.vector, ws_scales, "ws_plane")
+        sx_plane = scale_tile(nc.vector, sx_scales, "sx_plane")
+        wb_plane = scale_tile(nc.vector, wb_scales, "wb_plane")
+        ws = load_words(nc.sync, ws_words[0], "ws", U8)
+        sx = load_words(nc.sync, sx_words[0].rearrange("p c r -> p (c r)"), "sx", U32)
+        load_scales(sync4, ws_plane, ws_scales)
+        load_scales(sync4, sx_plane, sx_scales)
+        wb = load_words(nc.sync, wb_words[0], "wb", U8)
+        load_scales(sync4, wb_plane, wb_scales)
+        idx5 = load_list(offs5, "idx5")
+
+        pages = [sb.tile([P, E], F32, name=f"page{h}") for h in range(2)]
+        for page in pages:
+            nc.vector.memset(page[:], 0.0)
+
+        w = sb.tile([P, 2 * R], U8, name="w", align_bytes=64)
+        w_sc = sb.tile([P, R], U8, name="w_sc", align_bytes=64)
+        nc.scalar.copy(
+            out=w[:].bitcast(U16).rearrange("p (t m) -> p t m", t=PACK),
+            in_=w_raw[:].bitcast(U16).rearrange("p (m t) -> p t m", t=PACK),
+        )
+
+        picked = []
+        for name, lst in (("a", idx), ("b", idx2)):
+            sc = sb.tile([P, J], U8, name=f"x{name}_sc", align_bytes=64)
+            nc.vector.tensor_copy(sc[:], xt_plane[:].indirect(lst[:]))
+            picked.append(sc)
+        nc.vector.tensor_copy(
+            out=w_sc[:].rearrange("p (t m) -> p t m", t=PACK),
+            in_=w_plane[:].rearrange("p (m t) -> p t m", t=PACK),
+        )
+        words = []
+        for name, lst in (("a", idx), ("b", idx2)):
+            wd = sb.tile([P, J], U32, name=f"x{name}", align_bytes=64)
+            nc.vector.tensor_copy(wd[:], xt[:].indirect(lst[:]))
+            words.append(wd)
+
+        def first_product(side, t, bank):
+            nc.tensor.matmul_mx(
+                out=bank,
+                lhsT=w[:, 2 * P * t : 2 * P * (t + 1)].bitcast(E2M1),
+                lhsT_scale=w_sc[:, P * t : P * (t + 1)],
+                rhs=words[side][:].bitcast(E5M2),
+                rhs_scale=picked[side][:],
+                start=True,
+                stop=True,
+            )
+
+        def bank(name):
+            return psum.tile([P, J], F32, name=name, tag="bank", bufs=8)
+
+        whole = {}
+        a_looked = sb.tile([P, PACK, O], F32, name="a_looked")
+        diff = sb.tile([P, PACK, O], F32, name="diff")
+        for side, t in ((0, 0), (0, 1), (1, 0), (0, 2), (1, 1), (0, 3), (1, 2), (1, 3)):
+            acc = bank(f"acc{side}{t}")
+            first_product(side, t, acc[:])
+            whole[side, t] = sb.tile([P, J], F32, name=f"whole{side}{t}")
+            if (side, t) in ((1, 0), (1, 1), (1, 2), (1, 3)):
+                nc.vector.tensor_copy(out=whole[side, t][:], in_=acc[:])
+            else:
+                nc.scalar.copy(out=whole[side, t][:], in_=acc[:])
+            if side == 0:
+                nc.scalar.activation(a_looked[:, t, :], whole[0, t][:].indirect(idx3[:]), ACT.Copy)
+            else:
+                nc.vector.tensor_tensor(diff[:, t, :], whole[1, t][:].indirect(idx4[:]), a_looked[:, t, :], ALU.subtract)
+        p_banks = [bank(f"p_bank{h}") for h in range(2)]
+
+        hid = sb.tile([P, O, PACK], BF16, name="hid", align_bytes=64)
+        woven = diff[:].rearrange("p t o -> p o t")
+        half = O // 2
+        nc.scalar.activation(hid[:, :half, :], woven[:, :half, :], ACT.Abs)
+        nc.vector.scalar_tensor_tensor(hid[:, half:, :], woven[:, half:, :], -1.0, woven[:, half:, :], ALU.mult, ALU.max)
+        hq = sb.tile([P, O], U32, name="hq", align_bytes=64)
+        hq_sc = sb.tile([P, O], U8, name="hq_sc", align_bytes=64)
+        nc.vector.quantize_mx(out=hq[:].bitcast(E4M3), scales=hq_sc[:], in_=hid[:].rearrange("p o t -> p (o t)"))
+
+        def second_product(h, weight, weight_sc, moving, moving_sc, first):
+            nc.tensor.matmul_mx(
+                out=p_banks[h][:, 0:O],
+                lhsT=weight[:, 2 * P * h : 2 * P * (h + 1)].bitcast(E2M1),
+                lhsT_scale=weight_sc[:, P * h : P * (h + 1)],
+                rhs=moving[:].bitcast(E4M3),
+                rhs_scale=moving_sc[:],
+                start=first,
+                stop=not first,
+            )
+
+        for h in range(2):
+            second_product(h, ws, ws_plane, sx, sx_plane, True)
+        for h in range(2):
+            second_product(h, wb, wb_plane, hq, hq_sc, False)
+
+        res = [sb.tile([P, O], F32, name=f"res{h}") for h in range(2)]
+        nc.vector.tensor_copy(out=res[0][:], in_=p_banks[0][:, 0:O])
+        nc.vector.tensor_copy(pages[0][:].indirect(idx5[:]), res[0][:])
+        nc.sync.dma_start(out[0:P, :], pages[0][:])
+        nc.scalar.copy(out=res[1][:], in_=p_banks[1][:, 0:O])
+        nc.scalar.activation(pages[1][:].indirect(idx5[:]), res[1][:], ACT.Copy)
+        nc.scalar.dma_start(out[P : 2 * P, :], pages[1][:])

@@ -43,8 +43,8 @@ def tile_list_tied_looked_skip_scattered_kernel(
             queue.dma_start(tile[:].bitcast(I32), flat)
             return tile
 
-        def scale_tile(engine, src, name):
-            tile = sb.tile([P, src.shape[2]], U8, name=name, align_bytes=64)
+        def scale_tile(engine, width, name):
+            tile = sb.tile([P, width], U8, name=name, align_bytes=64)
             engine.memset(tile[:].bitcast(I32), 0)
             return tile
 
@@ -52,39 +52,41 @@ def tile_list_tied_looked_skip_scattered_kernel(
             for q in range(4):
                 queues[q].dma_start(tile[32 * q : 32 * q + 4, :].bitcast(I32), src[0, 4 * q : 4 * q + 4, :].bitcast(I32))
 
-        sync4 = [nc.sync] * 4
-        xt_plane = scale_tile(nc.vector, xt_scales, "xt_plane")
-        w_plane = scale_tile(nc.vector, w_scales, "w_plane")
-        idx = load_list(offs, "idx")
-        w_raw = load_words(nc.sync, w_words[0], "w_raw", U8)
-        idx2 = load_list(offs2, "idx2")
-        load_scales([nc.sync, nc.sync, nc.scalar, nc.scalar], xt_plane, xt_scales)
-        xt = load_words(nc.sync, xt_words[0].rearrange("p c r -> p (c r)"), "xt", U32)
-        load_scales(sync4, w_plane, w_scales)
-        idx3 = load_list(offs3, "idx3")
-        idx4 = load_list(offs4, "idx4")
-
-        ws_plane = scale_tile(nc.vector, ws_scales, "ws_plane")
-        sx_plane = scale_tile(nc.vector, sx_scales, "sx_plane")
-        wb_plane = scale_tile(nc.vector, wb_scales, "wb_plane")
-        ws = load_words(nc.sync, ws_words[0], "ws", U8)
-        sx = load_words(nc.sync, sx_words[0].rearrange("p c r -> p (c r)"), "sx", U32)
-        load_scales(sync4, ws_plane, ws_scales)
-        load_scales(sync4, sx_plane, sx_scales)
-        wb = load_words(nc.sync, wb_words[0], "wb", U8)
-        load_scales(sync4, wb_plane, wb_scales)
-        idx5 = load_list(offs5, "idx5")
-
+        xt_plane = scale_tile(nc.vector, T, "xt_plane")
         pages = [sb.tile([P, E], F32, name=f"page{h}") for h in range(2)]
         for page in pages:
             nc.vector.memset(page[:], 0.0)
+        w_plane = scale_tile(nc.vector, R, "w_plane")
+        late_plane = scale_tile(nc.vector, 2 * N + O, "late_plane")
+
+        idx = load_list(offs, "idx")
+        w_raw = sb.tile([P, 2 * R], U8, name="w_raw", tag="staged", align_bytes=64)
+        nc.sync.dma_start(w_raw[:].bitcast(I32), w_words[0].bitcast(I32))
+        idx2 = load_list(offs2, "idx2")
+        load_scales([nc.sync, nc.sync, nc.scalar, nc.scalar], xt_plane, xt_scales)
+        xt = load_words(nc.sync, xt_words[0].rearrange("p c r -> p (c r)"), "xt", U32)
+        load_scales([nc.scalar] * 4, w_plane, w_scales)
+        idx3 = load_list(offs3, "idx3")
+        idx4 = load_list(offs4, "idx4")
+        idx5 = load_list(offs5, "idx5")
 
         w = sb.tile([P, 2 * R], U8, name="w", align_bytes=64)
         w_sc = sb.tile([P, R], U8, name="w_sc", align_bytes=64)
-        nc.scalar.copy(
+        nc.vector.tensor_copy(
             out=w[:].bitcast(U16).rearrange("p (t m) -> p t m", t=PACK),
             in_=w_raw[:].bitcast(U16).rearrange("p (m t) -> p t m", t=PACK),
         )
+
+        late_words = sb.tile([P, 4 * N + 4 * O], U8, name="late_words", tag="staged", align_bytes=64)
+        ws, wb, sx = late_words[:, 0 : 2 * N], late_words[:, 2 * N : 4 * N], late_words[:, 4 * N :]
+        nc.sync.dma_start(ws.bitcast(I32), ws_words[0].bitcast(I32))
+        nc.sync.dma_start(sx.bitcast(I32), sx_words[0].rearrange("p c r -> p (c r)").bitcast(I32))
+        nc.sync.dma_start(wb.bitcast(I32), wb_words[0].bitcast(I32))
+        ws_plane, wb_plane, sx_plane = late_plane[:, 0:N], late_plane[:, N : 2 * N], late_plane[:, 2 * N :]
+        for plane, src in ((ws_plane, ws_scales), (sx_plane, sx_scales), (wb_plane, wb_scales)):
+            nc.sync.dma_start(plane[0:16, :].bitcast(I32), src[0].bitcast(I32))
+        for q in range(1, 4):
+            nc.sync.dma_start(late_plane[32 * q : 32 * q + 4, :].bitcast(I32), late_plane[4 * q : 4 * q + 4, :].bitcast(I32))
 
         picked = []
         for name, lst in (("a", idx), ("b", idx2)):
@@ -146,16 +148,16 @@ def tile_list_tied_looked_skip_scattered_kernel(
                 out=p_banks[h][:, 0:O],
                 lhsT=weight[:, 2 * P * h : 2 * P * (h + 1)].bitcast(E2M1),
                 lhsT_scale=weight_sc[:, P * h : P * (h + 1)],
-                rhs=moving[:].bitcast(E4M3),
-                rhs_scale=moving_sc[:],
+                rhs=moving.bitcast(E4M3),
+                rhs_scale=moving_sc,
                 start=first,
                 stop=not first,
             )
 
         for h in range(2):
-            second_product(h, ws, ws_plane, sx, sx_plane, True)
+            second_product(h, ws, ws_plane, sx.bitcast(U32), sx_plane, True)
         for h in range(2):
-            second_product(h, wb, wb_plane, hq, hq_sc, False)
+            second_product(h, wb, wb_plane, hq[:], hq_sc[:], False)
 
         res = [sb.tile([P, O], F32, name=f"res{h}") for h in range(2)]
         nc.vector.tensor_copy(out=res[0][:], in_=p_banks[0][:, 0:O])

@@ -53,55 +53,56 @@ def tile_list_tied_looked_skip_scattered_kernel(
                 queues[q].dma_start(tile[32 * q : 32 * q + 4, :].bitcast(I32), src[0, 4 * q : 4 * q + 4, :].bitcast(I32))
 
         xt_plane = scale_tile(nc.vector, T, "xt_plane")
+        w_plane = sb.tile([P, R], U8, name="w_plane", tag="w_plane_then_xb", align_bytes=64)
+        nc.vector.memset(w_plane[:].bitcast(I32), 0)
+        late_plane = scale_tile(nc.vector, 2 * N + O, "late_plane")
         pages = [sb.tile([P, E], F32, name=f"page{h}") for h in range(2)]
         for page in pages:
             nc.vector.memset(page[:], 0.0)
-        w_plane = scale_tile(nc.vector, R, "w_plane")
-        late_plane = scale_tile(nc.vector, 2 * N + O, "late_plane")
 
+        sync4 = [nc.sync] * 4
+        xt = sb.tile([P, T], U32, name="xt", align_bytes=64)
+        xt_src = xt_words[0].rearrange("p c r -> p (c r)").bitcast(I32)
+        nc.sync.dma_start(xt[:, : T // 2].bitcast(I32), xt_src[:, : T // 2])
         idx = load_list(offs, "idx")
-        w_raw = sb.tile([P, 2 * R], U8, name="w_raw", tag="staged", align_bytes=64)
-        nc.sync.dma_start(w_raw[:].bitcast(I32), w_words[0].bitcast(I32))
         idx2 = load_list(offs2, "idx2")
-        load_scales([nc.sync, nc.sync, nc.scalar, nc.scalar], xt_plane, xt_scales)
-        xt = load_words(nc.sync, xt_words[0].rearrange("p c r -> p (c r)"), "xt", U32)
-        load_scales([nc.scalar] * 4, w_plane, w_scales)
+        load_scales(sync4, xt_plane, xt_scales)
+        nc.sync.dma_start(xt[:, T // 2 :].bitcast(I32), xt_src[:, T // 2 :])
+        w_raw = load_words(nc.sync, w_words[0], "w_raw", U8)
+        load_scales(sync4, w_plane, w_scales)
         idx3 = load_list(offs3, "idx3")
         idx4 = load_list(offs4, "idx4")
-        idx5 = load_list(offs5, "idx5")
-
-        w = sb.tile([P, 2 * R], U8, name="w", align_bytes=64)
-        w_sc = sb.tile([P, R], U8, name="w_sc", align_bytes=64)
-        nc.vector.tensor_copy(
-            out=w[:].bitcast(U16).rearrange("p (t m) -> p t m", t=PACK),
-            in_=w_raw[:].bitcast(U16).rearrange("p (m t) -> p t m", t=PACK),
-        )
-
-        late_words = sb.tile([P, 4 * N + 4 * O], U8, name="late_words", tag="staged", align_bytes=64)
-        ws, wb, sx = late_words[:, 0 : 2 * N], late_words[:, 2 * N : 4 * N], late_words[:, 4 * N :]
-        nc.sync.dma_start(ws.bitcast(I32), ws_words[0].bitcast(I32))
-        nc.sync.dma_start(sx.bitcast(I32), sx_words[0].rearrange("p c r -> p (c r)").bitcast(I32))
-        nc.sync.dma_start(wb.bitcast(I32), wb_words[0].bitcast(I32))
         ws_plane, wb_plane, sx_plane = late_plane[:, 0:N], late_plane[:, N : 2 * N], late_plane[:, 2 * N :]
         for plane, src in ((ws_plane, ws_scales), (sx_plane, sx_scales), (wb_plane, wb_scales)):
             nc.sync.dma_start(plane[0:16, :].bitcast(I32), src[0].bitcast(I32))
+        ws = load_words(nc.sync, ws_words[0], "ws", U8)
+        sx = load_words(nc.sync, sx_words[0].rearrange("p c r -> p (c r)"), "sx", U32)
+        wb = load_words(nc.sync, wb_words[0], "wb", U8)
+        idx5 = load_list(offs5, "idx5")
         for q in range(1, 4):
             nc.sync.dma_start(late_plane[32 * q : 32 * q + 4, :].bitcast(I32), late_plane[4 * q : 4 * q + 4, :].bitcast(I32))
+
+        w = sb.tile([P, 2 * R], U8, name="w", align_bytes=64)
+        w_sc = sb.tile([P, R], U8, name="w_sc", align_bytes=64)
+        w_dealt = w[:].bitcast(U16).rearrange("p (t m) -> p t m", t=PACK)
+        w_natural = w_raw[:].bitcast(U16).rearrange("p (m t) -> p t m", t=PACK)
+        for u in range(2):
+            nc.scalar.copy(out=w_dealt[:, 2 * u : 2 * u + 2, :], in_=w_natural[:, 2 * u : 2 * u + 2, :])
 
         picked = []
         for name, lst in (("a", idx), ("b", idx2)):
             sc = sb.tile([P, J], U8, name=f"x{name}_sc", align_bytes=64)
             nc.vector.tensor_copy(sc[:], xt_plane[:].indirect(lst[:]))
             picked.append(sc)
+        xa = sb.tile([P, J], U32, name="xa", align_bytes=64)
+        nc.vector.tensor_copy(xa[:], xt[:].indirect(idx[:]))
         nc.vector.tensor_copy(
             out=w_sc[:].rearrange("p (t m) -> p t m", t=PACK),
             in_=w_plane[:].rearrange("p (m t) -> p t m", t=PACK),
         )
-        words = []
-        for name, lst in (("a", idx), ("b", idx2)):
-            wd = sb.tile([P, J], U32, name=f"x{name}", align_bytes=64)
-            nc.vector.tensor_copy(wd[:], xt[:].indirect(lst[:]))
-            words.append(wd)
+        xb = sb.tile([P, J], U32, name="xb", tag="w_plane_then_xb", align_bytes=64)
+        nc.vector.tensor_copy(xb[:], xt[:].indirect(idx2[:]))
+        words = [xa, xb]
 
         def first_product(side, t, bank):
             nc.tensor.matmul_mx(
@@ -155,7 +156,7 @@ def tile_list_tied_looked_skip_scattered_kernel(
             )
 
         for h in range(2):
-            second_product(h, ws, ws_plane, sx.bitcast(U32), sx_plane, True)
+            second_product(h, ws, ws_plane, sx[:], sx_plane, True)
         for h in range(2):
             second_product(h, wb, wb_plane, hq[:], hq_sc[:], False)
 

from contextlib import ExitStack

import concourse.mybir as mybir

K, T, J, R, O, N, L, E = 512, 2048, 256, 512, 128, 256, 512, 1024
FLOPS = 2 * (2 * K * R * J + R * N * O + L * N * O)

F32 = mybir.dt.float32
BF16 = mybir.dt.bfloat16
I32 = mybir.dt.int32
U32 = mybir.dt.uint32
U16 = mybir.dt.uint16
U8 = mybir.dt.uint8
E4M3 = mybir.dt.float8_e4m3fn_x4
E5M2 = mybir.dt.float8_e5m2_x4
E2M1 = mybir.dt.float4_e2m1fn_x4
ACT = mybir.ActivationFunctionType
ALU = mybir.AluOpType

P = 128
PACK = 4


def tile_list_tied_looked_skip_scattered_kernel(
    tc, xt_words, xt_scales, w_words, w_scales, wb_words, wb_scales, sx_words, sx_scales,
    ws_words, ws_scales, offs, offs2, offs3, offs4, offs5, out,
):
    nc = tc.nc
    with ExitStack() as ctx:
        lists = ctx.enter_context(tc.tile_pool(name="lists", bufs=1))
        sb = ctx.enter_context(tc.tile_pool(name="sb", bufs=1))
        psum = ctx.enter_context(tc.psum_pool(name="psum", bufs=1))

        def load_list(src, name):
            tile = lists.tile(list(src.shape), U16, name=name)
            nc.sync.dma_start(tile[:], src)
            return tile

        def load_words(queue, src, name, dtype):
            flat = src.bitcast(I32)
            per_word = 1 if dtype == U32 else 4
            tile = sb.tile([P, flat.shape[1] * per_word], dtype, name=name, align_bytes=64)
            queue.dma_start(tile[:].bitcast(I32), flat)
            return tile

        def scale_tile(engine, width, name):
            tile = sb.tile([P, width], U8, name=name, align_bytes=64)
            engine.memset(tile[:].bitcast(I32), 0)
            return tile

        def load_scales(queues, tile, src):
            for q in range(4):
                queues[q].dma_start(tile[32 * q : 32 * q + 4, :].bitcast(I32), src[0, 4 * q : 4 * q + 4, :].bitcast(I32))

        xt_plane = scale_tile(nc.vector, T, "xt_plane")
        w_plane = sb.tile([P, R], U8, name="w_plane", tag="w_plane_then_xb", align_bytes=64)
        nc.vector.memset(w_plane[:].bitcast(I32), 0)
        late_plane = scale_tile(nc.vector, 2 * N + O, "late_plane")
        pages = [sb.tile([P, E], F32, name=f"page{h}") for h in range(2)]
        for page in pages:
            nc.vector.memset(page[:], 0.0)

        sync4 = [nc.sync] * 4
        xt = sb.tile([P, T], U32, name="xt", align_bytes=64)
        xt_src = xt_words[0].rearrange("p c r -> p (c r)").bitcast(I32)
        nc.sync.dma_start(xt[:, : T // 2].bitcast(I32), xt_src[:, : T // 2])
        idx = load_list(offs, "idx")
        idx2 = load_list(offs2, "idx2")
        load_scales(sync4, xt_plane, xt_scales)
        nc.sync.dma_start(xt[:, T // 2 :].bitcast(I32), xt_src[:, T // 2 :])
        w_raw = load_words(nc.sync, w_words[0], "w_raw", U8)
        load_scales(sync4, w_plane, w_scales)
        idx3 = load_list(offs3, "idx3")
        idx4 = load_list(offs4, "idx4")
        ws_plane, wb_plane, sx_plane = late_plane[:, 0:N], late_plane[:, N : 2 * N], late_plane[:, 2 * N :]
        for plane, src in ((ws_plane, ws_scales), (sx_plane, sx_scales), (wb_plane, wb_scales)):
            nc.sync.dma_start(plane[0:16, :].bitcast(I32), src[0].bitcast(I32))
        ws = load_words(nc.sync, ws_words[0], "ws", U8)
        sx = load_words(nc.sync, sx_words[0].rearrange("p c r -> p (c r)"), "sx", U32)
        wb = load_words(nc.sync, wb_words[0], "wb", U8)
        idx5 = load_list(offs5, "idx5")
        for q in range(1, 4):
            nc.sync.dma_start(late_plane[32 * q : 32 * q + 4, :].bitcast(I32), late_plane[4 * q : 4 * q + 4, :].bitcast(I32))

        w = sb.tile([P, 2 * R], U8, name="w", align_bytes=64)
        w_sc = sb.tile([P, R], U8, name="w_sc", align_bytes=64)
        w_dealt = w[:].bitcast(U16).rearrange("p (t m) -> p t m", t=PACK)
        w_natural = w_raw[:].bitcast(U16).rearrange("p (m t) -> p t m", t=PACK)
        for u in range(2):
            nc.scalar.copy(out=w_dealt[:, 2 * u : 2 * u + 2, :], in_=w_natural[:, 2 * u : 2 * u + 2, :])

        picked = []
        for name, lst in (("a", idx), ("b", idx2)):
            sc = sb.tile([P, J], U8, name=f"x{name}_sc", align_bytes=64)
            nc.vector.tensor_copy(sc[:], xt_plane[:].indirect(lst[:]))
            picked.append(sc)
        xa = sb.tile([P, J], U32, name="xa", align_bytes=64)
        nc.vector.tensor_copy(xa[:], xt[:].indirect(idx[:]))
        nc.vector.tensor_copy(
            out=w_sc[:].rearrange("p (t m) -> p t m", t=PACK),
            in_=w_plane[:].rearrange("p (m t) -> p t m", t=PACK),
        )
        xb = sb.tile([P, J], U32, name="xb", tag="w_plane_then_xb", align_bytes=64)
        nc.vector.tensor_copy(xb[:], xt[:].indirect(idx2[:]))
        words = [xa, xb]

        def first_product(side, t, bank):
            nc.tensor.matmul_mx(
                out=bank,
                lhsT=w[:, 2 * P * t : 2 * P * (t + 1)].bitcast(E2M1),
                lhsT_scale=w_sc[:, P * t : P * (t + 1)],
                rhs=words[side][:].bitcast(E5M2),
                rhs_scale=picked[side][:],
                start=True,
                stop=True,
            )

        def bank(name):
            return psum.tile([P, J], F32, name=name, tag="bank", bufs=8)

        whole = {}
        a_looked = sb.tile([P, PACK, O], F32, name="a_looked")
        diff = sb.tile([P, PACK, O], F32, name="diff")
        for side, t in ((0, 0), (0, 1), (1, 0), (0, 2), (1, 1), (0, 3), (1, 2), (1, 3)):
            acc = bank(f"acc{side}{t}")
            first_product(side, t, acc[:])
            whole[side, t] = sb.tile([P, J], F32, name=f"whole{side}{t}")
            if (side, t) in ((1, 0), (1, 1), (1, 2), (1, 3)):
                nc.vector.tensor_copy(out=whole[side, t][:], in_=acc[:])
            else:
                nc.scalar.copy(out=whole[side, t][:], in_=acc[:])
            if side == 0:
                nc.scalar.activation(a_looked[:, t, :], whole[0, t][:].indirect(idx3[:]), ACT.Copy)
            else:
                nc.vector.tensor_tensor(diff[:, t, :], whole[1, t][:].indirect(idx4[:]), a_looked[:, t, :], ALU.subtract)
        p_banks = [bank(f"p_bank{h}") for h in range(2)]

        hid = sb.tile([P, O, PACK], BF16, name="hid", align_bytes=64)
        woven = diff[:].rearrange("p t o -> p o t")
        half = O // 2
        nc.scalar.activation(hid[:, :half, :], woven[:, :half, :], ACT.Abs)
        nc.vector.scalar_tensor_tensor(hid[:, half:, :], woven[:, half:, :], -1.0, woven[:, half:, :], ALU.mult, ALU.max)
        hq = sb.tile([P, O], U32, name="hq", align_bytes=64)
        hq_sc = sb.tile([P, O], U8, name="hq_sc", align_bytes=64)
        nc.vector.quantize_mx(out=hq[:].bitcast(E4M3), scales=hq_sc[:], in_=hid[:].rearrange("p o t -> p (o t)"))

        def second_product(h, weight, weight_sc, moving, moving_sc, first):
            nc.tensor.matmul_mx(
                out=p_banks[h][:, 0:O],
                lhsT=weight[:, 2 * P * h : 2 * P * (h + 1)].bitcast(E2M1),
                lhsT_scale=weight_sc[:, P * h : P * (h + 1)],
                rhs=moving.bitcast(E4M3),
                rhs_scale=moving_sc,
                start=first,
                stop=not first,
            )

        for h in range(2):
            second_product(h, ws, ws_plane, sx[:], sx_plane, True)
        for h in range(2):
            second_product(h, wb, wb_plane, hq[:], hq_sc[:], False)

        res = [sb.tile([P, O], F32, name=f"res{h}") for h in range(2)]
        nc.vector.tensor_copy(out=res[0][:], in_=p_banks[0][:, 0:O])
        nc.vector.tensor_copy(pages[0][:].indirect(idx5[:]), res[0][:])
        nc.sync.dma_start(out[0:P, :], pages[0][:])
        nc.scalar.copy(out=res[1][:], in_=p_banks[1][:, 0:O])
        nc.scalar.activation(pages[1][:].indirect(idx5[:]), res[1][:], ACT.Copy)
        nc.scalar.dma_start(out[P : 2 * P, :], pages[1][:])
